import numpy as np
import ml_dtypes


def mxq(x, axis, fmt="e4m3"):
    dtype, down = {"e4m3": (ml_dtypes.float8_e4m3fn, 7), "e5m2": (ml_dtypes.float8_e5m2, 14)}[fmt]
    v = np.moveaxis(np.asarray(x, np.float32).astype(ml_dtypes.bfloat16).astype(np.float64), axis, -1)
    blocks = v.reshape(v.shape[:-1] + (-1, 32))
    amax = np.abs(blocks).max(-1, keepdims=True)
    byte = np.maximum(np.where(amax > 0, np.frexp(amax)[1] - 1 + 127, 0) - down, 1)
    scale = np.exp2(byte - 127.0)
    codes = (blocks / scale).astype(np.float32).astype(dtype).astype(np.float64)
    return np.moveaxis((codes * scale).reshape(v.shape), -1, axis)


WIDE = False


def mx_kscale(k):
    if not WIDE:
        return np.ones(k)
    levels = np.array([10, -10, 5, -5, 0])
    if k % 512:
        return np.exp2(np.random.permutation(np.resize(levels, k // 32))).repeat(32)
    a = np.empty((k // 512, 16))
    for p in range(k // 512):
        a[p, :8] = np.random.permutation(np.resize(levels, 8))
        for g in range(8):
            far = levels[np.abs(levels - a[p, g]) >= 10]
            a[p, g + 8] = far[np.random.randint(len(far))]
    return np.exp2(a.ravel()).repeat(32)


def f64(x):
    return np.asarray(x).astype(np.float64)


def striped(idx):
    return np.tile(idx.reshape(-1, 16).T, (8, 1)).astype(np.uint16)


def unstriped(offs):
    return offs[:16].T.reshape(-1).astype(np.int64)


def striped8(idx):
    return np.concatenate([x.reshape(-1, 16).T for x in idx]).astype(np.uint16)


def runs(offs, k):
    lists = np.stack([offs[16 * r : 16 * r + 16].T.reshape(-1) for r in range(8)]).astype(np.int64)
    return lists[np.arange(k) % 512 // 64]


def pack_weight(w):
    k, n = w.shape
    w = f64(np.asarray(w, np.float32).astype(ml_dtypes.bfloat16)).reshape(k // 32, 32, n)
    amax = np.abs(w).max(1)
    byte = np.clip(np.where(amax > 0, np.frexp(amax)[1] - 1 + 127 - 7, 1), 1, 254)
    scaled = (w * np.exp2(127.0 - byte)[:, None, :]).reshape(k, n).astype(np.float32)
    words = np.ascontiguousarray(scaled.reshape(k // 512, 128, 4, n).transpose(0, 1, 3, 2)).astype(ml_dtypes.float8_e4m3fn).view(np.uint8)
    return words, np.ascontiguousarray(byte.astype(np.uint8).reshape(k // 512, 16, n))


def unpack_weight(words, scales):
    g, p, n, _ = words.shape
    vals = np.ascontiguousarray(words).view(ml_dtypes.float8_e4m3fn).astype(np.float64) * np.repeat(np.exp2(scales.astype(np.float64) - 127.0), 8, axis=1)[..., None]
    return vals.transpose(0, 1, 3, 2).reshape(g * 512, n)


def relu(v):
    return np.maximum(v, 0.0)


K, T, S, G, H = 512, 2048, 512, 2048, 512


def setup_inputs():
    n = np.random.standard_normal
    s = mx_kscale(K)[:, None]
    packed_xT = pack_weight(n((K, T)) * s)
    packed_dT = pack_weight(n((K, G)) / s)
    return {
        "x_words": packed_xT[0],
        "x_scales": packed_xT[1],
        "d_words": packed_dT[0],
        "d_scales": packed_dT[1],
        "gs": (np.random.uniform(0.5, 1.5, (K, 1)) * s).astype(np.float32),
        "offs": striped(np.random.permutation(T)[:S]),
        "k1": striped8(np.random.randint(0, G, (8, H))),
        "k2": striped8(np.random.randint(0, G, (8, H))),
    }


def reference(x_words, x_scales, d_words, d_scales, gs, offs, k1, k2):
    d_k2 = unpack_weight(d_words, d_scales)[np.arange(K)[:, None], runs(k2, K)]
    d_k1 = unpack_weight(d_words, d_scales)[np.arange(K)[:, None], runs(k1, K)]
    xq = unpack_weight(x_words, x_scales)[:, unstriped(offs)]
    h = relu(0.0625 * (d_k1.T @ xq))
    z = f64(gs) * h
    return 0.0625 * ((d_k2.T @ mxq(z, 0, "e4m3")))

@@ -1,0 +1,156 @@
+from contextlib import ExitStack
+
+import concourse.mybir as mybir
+
+K, T, S, G, H = 512, 2048, 512, 2048, 512
+FLOPS = 2 * K * H * S + 2 * H * H * S
+
+F32 = mybir.dt.float32
+BF16 = mybir.dt.bfloat16
+I32 = mybir.dt.int32
+U32 = mybir.dt.uint32
+U16 = mybir.dt.uint16
+U8 = mybir.dt.uint8
+FP8X4 = mybir.dt.float8_e4m3fn_x4
+ALU = mybir.AluOpType
+ACT = mybir.ActivationFunctionType
+
+P = 128
+PACK = 4
+CHUNK = 128
+HALF = 256
+SIXTEENTH = 0.0625
+
+
+def tile_picked_pqmlp2_relu_p_kernel(tc, x_words, x_scales, d_words, d_scales, gs, offs, k1, k2, out):
+    nc = tc.nc
+    with ExitStack() as ctx:
+        lists = ctx.enter_context(tc.tile_pool(name="lists", bufs=1))
+        keep = ctx.enter_context(tc.tile_pool(name="keep", bufs=1))
+        psum = ctx.enter_context(tc.psum_pool(name="psum", bufs=1))
+
+        k1_list = lists.tile([P, H // 16], U16, name="k1_list")
+        k2_list = lists.tile([P, H // 16], U16, name="k2_list")
+        x_list = lists.tile([P, S // 16], U16, name="x_list")
+
+        d_byte_table = keep.tile([P, G], U8, name="d_byte_table", align_bytes=64)
+        x_byte_table = keep.tile([P, T], U8, name="x_byte_table", align_bytes=64)
+        d_word_table = keep.tile([P, G], U32, name="d_word_table", align_bytes=64)
+        x_word_table = keep.tile([P, T], U32, name="x_word_table", align_bytes=64)
+        first_bytes = keep.tile([P, H + S], U8, name="first_bytes", align_bytes=64)
+        first_dealt = keep.tile([P, H + S], U8, name="first_dealt", align_bytes=64)
+        first_planes = keep.tile([P, H + S], U8, name="first_planes", align_bytes=64)
+        w2_bytes = keep.tile([P, H], U8, name="w2_bytes", align_bytes=64)
+        w2_plane = keep.tile([P, H], U8, name="w2_plane", align_bytes=64)
+        gain = keep.tile([P, PACK], F32, name="gain", align_bytes=64)
+        gain16 = keep.tile([P, PACK], F32, name="gain16", align_bytes=64)
+
+        nc.vector.memset(first_planes[:].bitcast(I32), 0)
+        nc.vector.memset(w2_plane[:].bitcast(I32), 0)
+
+        d_rows = d_scales[0].bitcast(I32)
+        x_rows = x_scales[0].bitcast(I32)
+        nc.sync.dma_start(k1_list[:], k1)
+        nc.sync.dma_start(d_byte_table[:].bitcast(I32), d_rows.unsqueeze(1).to_broadcast([16, 8, G // 4]))
+        nc.sync.dma_start(x_list[:], offs)
+        nc.sync.dma_start(x_byte_table[:].bitcast(I32), x_rows.unsqueeze(1).to_broadcast([16, 8, T // 4]))
+        nc.sync.dma_start(d_word_table[:].bitcast(I32), d_words[0].rearrange("p n t -> p (n t)").bitcast(I32))
+        nc.sync.dma_start(x_word_table[:].bitcast(I32), x_words[0].rearrange("p n t -> p (n t)").bitcast(I32))
+        nc.sync.dma_start(k2_list[:], k2)
+        nc.sync.dma_start(gain[:], gs.rearrange("(p t) o -> p (t o)", t=PACK))
+        nc.scalar.mul(gain16[:], gain[:], SIXTEENTH)
+
+        def place_rows(queue, planes, picked):
+            for j in range(PACK):
+                queue.dma_start(planes[j:P:32, :].bitcast(I32), picked[8 * j : P : 32, :].bitcast(I32))
+
+        nc.vector.tensor_copy(first_bytes[:, 0:H], d_byte_table[:].indirect(k1_list[:]))
+        nc.vector.tensor_copy(first_bytes[:, H : H + S], x_byte_table[:].indirect(x_list[:]))
+        nc.vector.tensor_copy(
+            first_dealt[:, 0:H].rearrange("p (t b i) -> p b t i", t=PACK, i=16),
+            first_bytes[:, 0:H].rearrange("p (b i t) -> p b t i", t=PACK, i=16),
+        )
+        nc.vector.tensor_copy(first_dealt[:, H : H + S].bitcast(I32), first_bytes[:, H : H + S].bitcast(I32))
+        place_rows(nc.scalar, first_planes, first_dealt)
+
+        w1_picked = keep.tile([P, H], U32, name="w1_picked", align_bytes=64)
+        w1_words = keep.tile([P, H], U32, name="w1_words", align_bytes=64)
+        w2_words = keep.tile([P, H], U32, name="w2_words", align_bytes=64)
+        x_picked = [keep.tile([P, HALF], U32, name="x_picked%d" % u, align_bytes=64) for u in range(2)]
+
+        def pick_words(u):
+            cols = slice(u * HALF // 16, (u + 1) * HALF // 16)
+            nc.vector.tensor_copy(x_picked[u][:], x_word_table[:].indirect(x_list[:, cols]))
+
+        nc.vector.tensor_copy(w1_picked[:], d_word_table[:].indirect(k1_list[:]))
+        nc.vector.tensor_copy(
+            w1_words[:].rearrange("p (t b i) -> p b t i", t=PACK, i=4),
+            w1_picked[:].rearrange("p (b i t) -> p b t i", t=PACK, i=4),
+        )
+        pick_words(0)
+
+        hidden = [psum.tile([P, PACK, CHUNK], F32, name="hidden%d" % c) for c in range(4)]
+        result = [psum.tile([P, PACK, CHUNK], F32, name="result%d" % c) for c in range(4)]
+        z = [keep.tile([P, CHUNK * PACK], BF16, name="z%d" % c, align_bytes=64) for c in range(4)]
+        z_words = [keep.tile([P, CHUNK], U32, name="z_words%d" % c, align_bytes=64) for c in range(4)]
+        z_plane = [keep.tile([P, CHUNK], U8, name="z_plane%d" % c, align_bytes=64) for c in range(4)]
+        staged = [keep.tile([P, PACK, CHUNK], F32, name="staged%d" % c, align_bytes=64) for c in range(4)]
+
+        def first_layer(c):
+            u, cols = c // 2, slice((c % 2) * CHUNK, (c % 2 + 1) * CHUNK)
+            for t in range(PACK):
+                rows = slice(t * P, (t + 1) * P)
+                nc.tensor.matmul_mx(
+                    out=hidden[c][:, t, :],
+                    lhsT=w1_words[:, rows].bitcast(FP8X4),
+                    lhsT_scale=first_planes[:, rows],
+                    rhs=x_picked[u][:, cols].bitcast(FP8X4),
+                    rhs_scale=first_planes[:, H + c * CHUNK : H + (c + 1) * CHUNK],
+                    start=True,
+                    stop=True,
+                )
+
+        def weigh(c):
+            nc.vector.scalar_tensor_tensor(
+                out=z[c][:].rearrange("p (n t) -> p n t", t=PACK),
+                in0=hidden[c][:].rearrange("p t n -> p n t"),
+                scalar=0.0,
+                in1=gain16[:].unsqueeze(1).to_broadcast([P, CHUNK, PACK]),
+                op0=ALU.max,
+                op1=ALU.mult,
+            )
+
+        def quantise(c):
+            nc.vector.quantize_mx(out=z_words[c][:].bitcast(FP8X4), scales=z_plane[c][:], in_=z[c][:])
+
+        def second_layer(c):
+            for b in range(PACK):
+                rows = slice(b * P, (b + 1) * P)
+                nc.tensor.matmul_mx(
+                    out=result[c][:, b, :],
+                    lhsT=w2_words[:, rows].bitcast(FP8X4),
+                    lhsT_scale=w2_plane[:, rows],
+                    rhs=z_words[c][:].bitcast(FP8X4),
+                    rhs_scale=z_plane[c][:],
+                    start=True,
+                    stop=True,
+                )
+            nc.scalar.mul(staged[c][:], result[c][:], SIXTEENTH)
+            nc.sync.dma_start(
+                out[:, c * CHUNK : (c + 1) * CHUNK].rearrange("(b p) n -> p b n", p=P), staged[c][:]
+            )
+
+        first_layer(0)
+        first_layer(1)
+        pick_words(1)
+        first_layer(2)
+        first_layer(3)
+        nc.vector.tensor_copy(w2_bytes[:], d_byte_table[:].indirect(k2_list[:]))
+        place_rows(nc.sync, w2_plane, w2_bytes)
+        nc.vector.tensor_copy(w2_words[:], d_word_table[:].indirect(k2_list[:]))
+        weigh(0)
+        for c in range(4):
+            if c + 1 < 4:
+                weigh(c + 1)
+            quantise(c)
+            second_layer(c)

@@ -45,6 +45,7 @@ def tile_picked_pqmlp2_relu_p_kernel(tc, x_words, x_scales, d_words, d_scales, g
         gain = keep.tile([P, PACK], F32, name="gain", align_bytes=64)
         gain16 = keep.tile([P, PACK], F32, name="gain16", align_bytes=64)
 
+        nc.vector.memset(x_byte_table[:].bitcast(I32), 0)
         nc.vector.memset(first_planes[:].bitcast(I32), 0)
         nc.vector.memset(w2_plane[:].bitcast(I32), 0)
 
@@ -53,11 +54,11 @@ def tile_picked_pqmlp2_relu_p_kernel(tc, x_words, x_scales, d_words, d_scales, g
         nc.sync.dma_start(k1_list[:], k1)
         nc.sync.dma_start(d_byte_table[:].bitcast(I32), d_rows.unsqueeze(1).to_broadcast([16, 8, G // 4]))
         nc.sync.dma_start(x_list[:], offs)
-        nc.sync.dma_start(x_byte_table[:].bitcast(I32), x_rows.unsqueeze(1).to_broadcast([16, 8, T // 4]))
+        nc.sync.dma_start(gain[:], gs.rearrange("(p t) o -> p (t o)", t=PACK))
+        nc.sync.dma_start(x_byte_table[0:P:8, :].bitcast(I32), x_rows)
         nc.sync.dma_start(d_word_table[:].bitcast(I32), d_words[0].rearrange("p n t -> p (n t)").bitcast(I32))
         nc.sync.dma_start(x_word_table[:].bitcast(I32), x_words[0].rearrange("p n t -> p (n t)").bitcast(I32))
         nc.sync.dma_start(k2_list[:], k2)
-        nc.sync.dma_start(gain[:], gs.rearrange("(p t) o -> p (t o)", t=PACK))
         nc.scalar.mul(gain16[:], gain[:], SIXTEENTH)
 
         def place_rows(queue, planes, picked):
@@ -75,7 +76,6 @@ def tile_picked_pqmlp2_relu_p_kernel(tc, x_words, x_scales, d_words, d_scales, g
 
         w1_picked = keep.tile([P, H], U32, name="w1_picked", align_bytes=64)
         w1_words = keep.tile([P, H], U32, name="w1_words", align_bytes=64)
-        w2_words = keep.tile([P, H], U32, name="w2_words", align_bytes=64)
         x_picked = [keep.tile([P, HALF], U32, name="x_picked%d" % u, align_bytes=64) for u in range(2)]
 
         def pick_words(u):
@@ -94,7 +94,7 @@ def tile_picked_pqmlp2_relu_p_kernel(tc, x_words, x_scales, d_words, d_scales, g
         z = [keep.tile([P, CHUNK * PACK], BF16, name="z%d" % c, align_bytes=64) for c in range(4)]
         z_words = [keep.tile([P, CHUNK], U32, name="z_words%d" % c, align_bytes=64) for c in range(4)]
         z_plane = [keep.tile([P, CHUNK], U8, name="z_plane%d" % c, align_bytes=64) for c in range(4)]
-        staged = [keep.tile([P, PACK, CHUNK], F32, name="staged%d" % c, align_bytes=64) for c in range(4)]
+        staged = [keep.tile([P, PACK, CHUNK], F32, name="staged%d" % c, align_bytes=64) for c in range(2)]
 
         def first_layer(c):
             u, cols = c // 2, slice((c % 2) * CHUNK, (c % 2 + 1) * CHUNK)
@@ -123,11 +123,11 @@ def tile_picked_pqmlp2_relu_p_kernel(tc, x_words, x_scales, d_words, d_scales, g
         def quantise(c):
             nc.vector.quantize_mx(out=z_words[c][:].bitcast(FP8X4), scales=z_plane[c][:], in_=z[c][:])
 
-        def second_layer(c):
-            for b in range(PACK):
+        def products(c, bank, blocks):
+            for slot, b in enumerate(blocks):
                 rows = slice(b * P, (b + 1) * P)
                 nc.tensor.matmul_mx(
-                    out=result[c][:, b, :],
+                    out=bank[:, slot, :],
                     lhsT=w2_words[:, rows].bitcast(FP8X4),
                     lhsT_scale=w2_plane[:, rows],
                     rhs=z_words[c][:].bitcast(FP8X4),
@@ -135,10 +135,26 @@ def tile_picked_pqmlp2_relu_p_kernel(tc, x_words, x_scales, d_words, d_scales, g
                     start=True,
                     stop=True,
                 )
+
+        def store(c, tile, first, count):
+            rows = out[first * P : (first + count) * P, c * CHUNK : (c + 1) * CHUNK]
+            nc.sync.dma_start(rows.rearrange("(b p) n -> p b n", p=P), tile[:])
+
+        def second_layer(c):
+            products(c, result[c], range(PACK))
             nc.scalar.mul(staged[c][:], result[c][:], SIXTEENTH)
-            nc.sync.dma_start(
-                out[:, c * CHUNK : (c + 1) * CHUNK].rearrange("(b p) n -> p b n", p=P), staged[c][:]
-            )
+            store(c, staged[c], 0, PACK)
+
+        def last_second_layer(c):
+            upper = psum.tile([P, 2, CHUNK], F32, name="upper%d" % c, tag="hidden%d" % (c - 2))
+            low_staged = keep.tile([P, 2, CHUNK], F32, name="low_staged%d" % c, align_bytes=64)
+            up_staged = keep.tile([P, 2, CHUNK], F32, name="up_staged%d" % c, align_bytes=64)
+            products(c, result[c], (0, 1))
+            products(c, upper, (2, 3))
+            nc.vector.tensor_scalar_mul(low_staged[:], result[c][:, 0:2, :], SIXTEENTH)
+            store(c, low_staged, 0, 2)
+            nc.scalar.mul(up_staged[:], upper[:], SIXTEENTH)
+            store(c, up_staged, 2, 2)
 
         first_layer(0)
         first_layer(1)
@@ -147,10 +163,17 @@ def tile_picked_pqmlp2_relu_p_kernel(tc, x_words, x_scales, d_words, d_scales, g
         first_layer(3)
         nc.vector.tensor_copy(w2_bytes[:], d_byte_table[:].indirect(k2_list[:]))
         place_rows(nc.sync, w2_plane, w2_bytes)
+        w2_words = keep.tile([P, H], U32, name="w2_words", align_bytes=64)
         nc.vector.tensor_copy(w2_words[:], d_word_table[:].indirect(k2_list[:]))
         weigh(0)
-        for c in range(4):
-            if c + 1 < 4:
-                weigh(c + 1)
-            quantise(c)
-            second_layer(c)
+        weigh(1)
+        quantise(0)
+        quantise(1)
+        second_layer(0)
+        second_layer(1)
+        weigh(2)
+        weigh(3)
+        quantise(2)
+        quantise(3)
+        last_second_layer(2)
+        last_second_layer(3)

@@ -76,7 +76,7 @@ def tile_picked_pqmlp2_relu_p_kernel(tc, x_words, x_scales, d_words, d_scales, g
 
         w1_picked = keep.tile([P, H], U32, name="w1_picked", align_bytes=64)
         w1_words = keep.tile([P, H], U32, name="w1_words", align_bytes=64)
-        x_picked = [keep.tile([P, HALF], U32, name="x_picked%d" % u, align_bytes=64) for u in range(2)]
+        x_picked = [keep.tile([P, HALF], U32, name="x_picked%d" % u, align_bytes=64) for u in range(1)]
 
         def pick_words(u):
             cols = slice(u * HALF // 16, (u + 1) * HALF // 16)
@@ -90,11 +90,9 @@ def tile_picked_pqmlp2_relu_p_kernel(tc, x_words, x_scales, d_words, d_scales, g
         pick_words(0)
 
         hidden = [psum.tile([P, PACK, CHUNK], F32, name="hidden%d" % c) for c in range(4)]
-        result = [psum.tile([P, PACK, CHUNK], F32, name="result%d" % c) for c in range(4)]
         z = [keep.tile([P, CHUNK * PACK], BF16, name="z%d" % c, align_bytes=64) for c in range(4)]
         z_words = [keep.tile([P, CHUNK], U32, name="z_words%d" % c, align_bytes=64) for c in range(4)]
         z_plane = [keep.tile([P, CHUNK], U8, name="z_plane%d" % c, align_bytes=64) for c in range(4)]
-        staged = [keep.tile([P, PACK, CHUNK], F32, name="staged%d" % c, align_bytes=64) for c in range(2)]
 
         def first_layer(c):
             u, cols = c // 2, slice((c % 2) * CHUNK, (c % 2 + 1) * CHUNK)
@@ -123,48 +121,40 @@ def tile_picked_pqmlp2_relu_p_kernel(tc, x_words, x_scales, d_words, d_scales, g
         def quantise(c):
             nc.vector.quantize_mx(out=z_words[c][:].bitcast(FP8X4), scales=z_plane[c][:], in_=z[c][:])
 
-        def products(c, bank, blocks):
-            for slot, b in enumerate(blocks):
-                rows = slice(b * P, (b + 1) * P)
-                nc.tensor.matmul_mx(
-                    out=bank[:, slot, :],
-                    lhsT=w2_words[:, rows].bitcast(FP8X4),
-                    lhsT_scale=w2_plane[:, rows],
-                    rhs=z_words[c][:].bitcast(FP8X4),
-                    rhs_scale=z_plane[c][:],
-                    start=True,
-                    stop=True,
-                )
-
-        def store(c, tile, first, count):
-            rows = out[first * P : (first + count) * P, c * CHUNK : (c + 1) * CHUNK]
-            nc.sync.dma_start(rows.rearrange("(b p) n -> p b n", p=P), tile[:])
-
         def second_layer(c):
-            products(c, result[c], range(PACK))
-            nc.scalar.mul(staged[c][:], result[c][:], SIXTEENTH)
-            store(c, staged[c], 0, PACK)
-
-        def last_second_layer(c):
-            upper = psum.tile([P, 2, CHUNK], F32, name="upper%d" % c, tag="hidden%d" % (c - 2))
-            low_staged = keep.tile([P, 2, CHUNK], F32, name="low_staged%d" % c, align_bytes=64)
-            up_staged = keep.tile([P, 2, CHUNK], F32, name="up_staged%d" % c, align_bytes=64)
-            products(c, result[c], (0, 1))
-            products(c, upper, (2, 3))
-            nc.vector.tensor_scalar_mul(low_staged[:], result[c][:, 0:2, :], SIXTEENTH)
-            store(c, low_staged, 0, 2)
-            nc.scalar.mul(up_staged[:], upper[:], SIXTEENTH)
-            store(c, up_staged, 2, 2)
+            for half in range(2):
+                slot = 2 * c + half
+                tag = "result%d" % slot if slot < 4 else "hidden%d" % (slot - 4)
+                bank = psum.tile([P, 2, CHUNK], F32, name="bank%d" % slot, tag=tag)
+                staged = keep.tile([P, 2, CHUNK], F32, name="staged%d" % slot, align_bytes=64)
+                for b in range(2):
+                    rows = slice((2 * half + b) * P, (2 * half + b + 1) * P)
+                    nc.tensor.matmul_mx(
+                        out=bank[:, b, :],
+                        lhsT=w2_words[:, rows].bitcast(FP8X4),
+                        lhsT_scale=w2_plane[:, rows],
+                        rhs=z_words[c][:].bitcast(FP8X4),
+                        rhs_scale=z_plane[c][:],
+                        start=True,
+                        stop=True,
+                    )
+                if c >= 2 and half == 0:
+                    nc.vector.tensor_scalar_mul(staged[:], bank[:], SIXTEENTH)
+                else:
+                    nc.scalar.mul(staged[:], bank[:], SIXTEENTH)
+                rows = out[2 * half * P : 2 * (half + 1) * P, c * CHUNK : (c + 1) * CHUNK]
+                nc.sync.dma_start(rows.rearrange("(b p) n -> p b n", p=P), staged[:])
 
         first_layer(0)
         first_layer(1)
-        pick_words(1)
-        first_layer(2)
-        first_layer(3)
         nc.vector.tensor_copy(w2_bytes[:], d_byte_table[:].indirect(k2_list[:]))
         place_rows(nc.sync, w2_plane, w2_bytes)
         w2_words = keep.tile([P, H], U32, name="w2_words", align_bytes=64)
         nc.vector.tensor_copy(w2_words[:], d_word_table[:].indirect(k2_list[:]))
+        x_picked.append(keep.tile([P, HALF], U32, name="x_picked1", tag="d_byte_table", align_bytes=64))
+        pick_words(1)
+        first_layer(2)
+        first_layer(3)
         weigh(0)
         weigh(1)
         quantise(0)
@@ -175,5 +165,5 @@ def tile_picked_pqmlp2_relu_p_kernel(tc, x_words, x_scales, d_words, d_scales, g
         weigh(3)
         quantise(2)
         quantise(3)
-        last_second_layer(2)
-        last_second_layer(3)
+        second_layer(2)
+        second_layer(3)

@@ -54,11 +54,11 @@ def tile_picked_pqmlp2_relu_p_kernel(tc, x_words, x_scales, d_words, d_scales, g
         nc.sync.dma_start(k1_list[:], k1)
         nc.sync.dma_start(d_byte_table[:].bitcast(I32), d_rows.unsqueeze(1).to_broadcast([16, 8, G // 4]))
         nc.sync.dma_start(x_list[:], offs)
-        nc.sync.dma_start(gain[:], gs.rearrange("(p t) o -> p (t o)", t=PACK))
+        nc.sync.dma_start(k2_list[:], k2)
         nc.sync.dma_start(x_byte_table[0:P:8, :].bitcast(I32), x_rows)
         nc.sync.dma_start(d_word_table[:].bitcast(I32), d_words[0].rearrange("p n t -> p (n t)").bitcast(I32))
         nc.sync.dma_start(x_word_table[:].bitcast(I32), x_words[0].rearrange("p n t -> p (n t)").bitcast(I32))
-        nc.sync.dma_start(k2_list[:], k2)
+        nc.sync.dma_start(gain[:], gs.rearrange("(p t) o -> p (t o)", t=PACK))
         nc.scalar.mul(gain16[:], gain[:], SIXTEENTH)
 
         def place_rows(queue, planes, picked):
@@ -73,10 +73,12 @@ def tile_picked_pqmlp2_relu_p_kernel(tc, x_words, x_scales, d_words, d_scales, g
         )
         nc.vector.tensor_copy(first_dealt[:, H : H + S].bitcast(I32), first_bytes[:, H : H + S].bitcast(I32))
         place_rows(nc.scalar, first_planes, first_dealt)
+        nc.vector.tensor_copy(w2_bytes[:], d_byte_table[:].indirect(k2_list[:]))
+        place_rows(nc.sync, w2_plane, w2_bytes)
 
         w1_picked = keep.tile([P, H], U32, name="w1_picked", align_bytes=64)
         w1_words = keep.tile([P, H], U32, name="w1_words", align_bytes=64)
-        x_picked = [keep.tile([P, HALF], U32, name="x_picked%d" % u, align_bytes=64) for u in range(1)]
+        x_picked = [keep.tile([P, HALF], U32, name="x_picked%d" % u, align_bytes=64) for u in range(2)]
 
         def pick_words(u):
             cols = slice(u * HALF // 16, (u + 1) * HALF // 16)
@@ -147,14 +149,11 @@ def tile_picked_pqmlp2_relu_p_kernel(tc, x_words, x_scales, d_words, d_scales, g
 
         first_layer(0)
         first_layer(1)
-        nc.vector.tensor_copy(w2_bytes[:], d_byte_table[:].indirect(k2_list[:]))
-        place_rows(nc.sync, w2_plane, w2_bytes)
-        w2_words = keep.tile([P, H], U32, name="w2_words", align_bytes=64)
-        nc.vector.tensor_copy(w2_words[:], d_word_table[:].indirect(k2_list[:]))
-        x_picked.append(keep.tile([P, HALF], U32, name="x_picked1", tag="d_byte_table", align_bytes=64))
         pick_words(1)
         first_layer(2)
         first_layer(3)
+        w2_words = keep.tile([P, H], U32, name="w2_words", tag="gain", align_bytes=64)
+        nc.vector.tensor_copy(w2_words[:], d_word_table[:].indirect(k2_list[:]))
         weigh(0)
         weigh(1)
         quantise(0)

@@ -40,7 +40,6 @@ def tile_picked_pqmlp2_relu_p_kernel(tc, x_words, x_scales, d_words, d_scales, g
         first_bytes = keep.tile([P, H + S], U8, name="first_bytes", align_bytes=64)
         first_dealt = keep.tile([P, H + S], U8, name="first_dealt", align_bytes=64)
         first_planes = keep.tile([P, H + S], U8, name="first_planes", align_bytes=64)
-        w2_bytes = keep.tile([P, H], U8, name="w2_bytes", align_bytes=64)
         w2_plane = keep.tile([P, H], U8, name="w2_plane", align_bytes=64)
         gain = keep.tile([P, PACK], F32, name="gain", align_bytes=64)
         gain16 = keep.tile([P, PACK], F32, name="gain16", align_bytes=64)
@@ -73,6 +72,7 @@ def tile_picked_pqmlp2_relu_p_kernel(tc, x_words, x_scales, d_words, d_scales, g
         )
         nc.vector.tensor_copy(first_dealt[:, H : H + S].bitcast(I32), first_bytes[:, H : H + S].bitcast(I32))
         place_rows(nc.scalar, first_planes, first_dealt)
+        w2_bytes = keep.tile([P, H], U8, name="w2_bytes", tag="x_byte_table", align_bytes=64)
         nc.vector.tensor_copy(w2_bytes[:], d_byte_table[:].indirect(k2_list[:]))
         place_rows(nc.sync, w2_plane, w2_bytes)
 

from contextlib import ExitStack

import concourse.mybir as mybir

K, T, S, G, H = 512, 2048, 512, 2048, 512
FLOPS = 2 * K * H * S + 2 * H * H * S

F32 = mybir.dt.float32
BF16 = mybir.dt.bfloat16
I32 = mybir.dt.int32
U32 = mybir.dt.uint32
U16 = mybir.dt.uint16
U8 = mybir.dt.uint8
FP8X4 = mybir.dt.float8_e4m3fn_x4
ALU = mybir.AluOpType
ACT = mybir.ActivationFunctionType

P = 128
PACK = 4
CHUNK = 128
HALF = 256
SIXTEENTH = 0.0625


def tile_picked_pqmlp2_relu_p_kernel(tc, x_words, x_scales, d_words, d_scales, gs, offs, k1, k2, out):
    nc = tc.nc
    with ExitStack() as ctx:
        lists = ctx.enter_context(tc.tile_pool(name="lists", bufs=1))
        keep = ctx.enter_context(tc.tile_pool(name="keep", bufs=1))
        psum = ctx.enter_context(tc.psum_pool(name="psum", bufs=1))

        k1_list = lists.tile([P, H // 16], U16, name="k1_list")
        k2_list = lists.tile([P, H // 16], U16, name="k2_list")
        x_list = lists.tile([P, S // 16], U16, name="x_list")

        d_byte_table = keep.tile([P, G], U8, name="d_byte_table", align_bytes=64)
        x_byte_table = keep.tile([P, T], U8, name="x_byte_table", align_bytes=64)
        d_word_table = keep.tile([P, G], U32, name="d_word_table", align_bytes=64)
        x_word_table = keep.tile([P, T], U32, name="x_word_table", align_bytes=64)
        first_bytes = keep.tile([P, H + S], U8, name="first_bytes", align_bytes=64)
        first_dealt = keep.tile([P, H + S], U8, name="first_dealt", align_bytes=64)
        first_planes = keep.tile([P, H + S], U8, name="first_planes", align_bytes=64)
        w2_plane = keep.tile([P, H], U8, name="w2_plane", align_bytes=64)
        gain = keep.tile([P, PACK], F32, name="gain", align_bytes=64)
        gain16 = keep.tile([P, PACK], F32, name="gain16", align_bytes=64)

        nc.vector.memset(x_byte_table[:].bitcast(I32), 0)
        nc.vector.memset(first_planes[:].bitcast(I32), 0)
        nc.vector.memset(w2_plane[:].bitcast(I32), 0)

        d_rows = d_scales[0].bitcast(I32)
        x_rows = x_scales[0].bitcast(I32)
        nc.sync.dma_start(k1_list[:], k1)
        nc.sync.dma_start(d_byte_table[:].bitcast(I32), d_rows.unsqueeze(1).to_broadcast([16, 8, G // 4]))
        nc.sync.dma_start(x_list[:], offs)
        nc.sync.dma_start(k2_list[:], k2)
        nc.sync.dma_start(x_byte_table[0:P:8, :].bitcast(I32), x_rows)
        nc.sync.dma_start(d_word_table[:].bitcast(I32), d_words[0].rearrange("p n t -> p (n t)").bitcast(I32))
        nc.sync.dma_start(x_word_table[:].bitcast(I32), x_words[0].rearrange("p n t -> p (n t)").bitcast(I32))
        nc.sync.dma_start(gain[:], gs.rearrange("(p t) o -> p (t o)", t=PACK))
        nc.scalar.mul(gain16[:], gain[:], SIXTEENTH)

        def place_rows(queue, planes, picked):
            for j in range(PACK):
                queue.dma_start(planes[j:P:32, :].bitcast(I32), picked[8 * j : P : 32, :].bitcast(I32))

        nc.vector.tensor_copy(first_bytes[:, 0:H], d_byte_table[:].indirect(k1_list[:]))
        nc.vector.tensor_copy(first_bytes[:, H : H + S], x_byte_table[:].indirect(x_list[:]))
        nc.vector.tensor_copy(
            first_dealt[:, 0:H].rearrange("p (t b i) -> p b t i", t=PACK, i=16),
            first_bytes[:, 0:H].rearrange("p (b i t) -> p b t i", t=PACK, i=16),
        )
        nc.vector.tensor_copy(first_dealt[:, H : H + S].bitcast(I32), first_bytes[:, H : H + S].bitcast(I32))
        place_rows(nc.scalar, first_planes, first_dealt)
        w2_bytes = keep.tile([P, H], U8, name="w2_bytes", tag="x_byte_table", align_bytes=64)
        nc.vector.tensor_copy(w2_bytes[:], d_byte_table[:].indirect(k2_list[:]))
        place_rows(nc.sync, w2_plane, w2_bytes)

        w1_picked = keep.tile([P, H], U32, name="w1_picked", align_bytes=64)
        w1_words = keep.tile([P, H], U32, name="w1_words", align_bytes=64)
        x_picked = [keep.tile([P, HALF], U32, name="x_picked%d" % u, align_bytes=64) for u in range(2)]

        def pick_words(u):
            cols = slice(u * HALF // 16, (u + 1) * HALF // 16)
            nc.vector.tensor_copy(x_picked[u][:], x_word_table[:].indirect(x_list[:, cols]))

        nc.vector.tensor_copy(w1_picked[:], d_word_table[:].indirect(k1_list[:]))
        nc.vector.tensor_copy(
            w1_words[:].rearrange("p (t b i) -> p b t i", t=PACK, i=4),
            w1_picked[:].rearrange("p (b i t) -> p b t i", t=PACK, i=4),
        )
        pick_words(0)

        hidden = [psum.tile([P, PACK, CHUNK], F32, name="hidden%d" % c) for c in range(4)]
        z = [keep.tile([P, CHUNK * PACK], BF16, name="z%d" % c, align_bytes=64) for c in range(4)]
        z_words = [keep.tile([P, CHUNK], U32, name="z_words%d" % c, align_bytes=64) for c in range(4)]
        z_plane = [keep.tile([P, CHUNK], U8, name="z_plane%d" % c, align_bytes=64) for c in range(4)]

        def first_layer(c):
            u, cols = c // 2, slice((c % 2) * CHUNK, (c % 2 + 1) * CHUNK)
            for t in range(PACK):
                rows = slice(t * P, (t + 1) * P)
                nc.tensor.matmul_mx(
                    out=hidden[c][:, t, :],
                    lhsT=w1_words[:, rows].bitcast(FP8X4),
                    lhsT_scale=first_planes[:, rows],
                    rhs=x_picked[u][:, cols].bitcast(FP8X4),
                    rhs_scale=first_planes[:, H + c * CHUNK : H + (c + 1) * CHUNK],
                    start=True,
                    stop=True,
                )

        def weigh(c):
            nc.vector.scalar_tensor_tensor(
                out=z[c][:].rearrange("p (n t) -> p n t", t=PACK),
                in0=hidden[c][:].rearrange("p t n -> p n t"),
                scalar=0.0,
                in1=gain16[:].unsqueeze(1).to_broadcast([P, CHUNK, PACK]),
                op0=ALU.max,
                op1=ALU.mult,
            )

        def quantise(c):
            nc.vector.quantize_mx(out=z_words[c][:].bitcast(FP8X4), scales=z_plane[c][:], in_=z[c][:])

        def second_layer(c):
            for half in range(2):
                slot = 2 * c + half
                tag = "result%d" % slot if slot < 4 else "hidden%d" % (slot - 4)
                bank = psum.tile([P, 2, CHUNK], F32, name="bank%d" % slot, tag=tag)
                staged = keep.tile([P, 2, CHUNK], F32, name="staged%d" % slot, align_bytes=64)
                for b in range(2):
                    rows = slice((2 * half + b) * P, (2 * half + b + 1) * P)
                    nc.tensor.matmul_mx(
                        out=bank[:, b, :],
                        lhsT=w2_words[:, rows].bitcast(FP8X4),
                        lhsT_scale=w2_plane[:, rows],
                        rhs=z_words[c][:].bitcast(FP8X4),
                        rhs_scale=z_plane[c][:],
                        start=True,
                        stop=True,
                    )
                if c >= 2 and half == 0:
                    nc.vector.tensor_scalar_mul(staged[:], bank[:], SIXTEENTH)
                else:
                    nc.scalar.mul(staged[:], bank[:], SIXTEENTH)
                rows = out[2 * half * P : 2 * (half + 1) * P, c * CHUNK : (c + 1) * CHUNK]
                nc.sync.dma_start(rows.rearrange("(b p) n -> p b n", p=P), staged[:])

        first_layer(0)
        first_layer(1)
        pick_words(1)
        first_layer(2)
        first_layer(3)
        w2_words = keep.tile([P, H], U32, name="w2_words", tag="gain", align_bytes=64)
        nc.vector.tensor_copy(w2_words[:], d_word_table[:].indirect(k2_list[:]))
        weigh(0)
        weigh(1)
        quantise(0)
        quantise(1)
        second_layer(0)
        second_layer(1)
        weigh(2)
        weigh(3)
        quantise(2)
        quantise(3)
        second_layer(2)
        second_layer(3)
